import numpy as np
import ml_dtypes


def mxq(x, axis, fmt="e4m3"):
    dtype, down = {"e4m3": (ml_dtypes.float8_e4m3fn, 7), "e5m2": (ml_dtypes.float8_e5m2, 14)}[fmt]
    v = np.moveaxis(np.asarray(x, np.float32).astype(ml_dtypes.bfloat16).astype(np.float64), axis, -1)
    blocks = v.reshape(v.shape[:-1] + (-1, 32))
    amax = np.abs(blocks).max(-1, keepdims=True)
    byte = np.maximum(np.where(amax > 0, np.frexp(amax)[1] - 1 + 127, 0) - down, 1)
    scale = np.exp2(byte - 127.0)
    codes = (blocks / scale).astype(np.float32).astype(dtype).astype(np.float64)
    return np.moveaxis((codes * scale).reshape(v.shape), -1, axis)


WIDE = False


def mx_kscale(k):
    if not WIDE:
        return np.ones(k)
    levels = np.array([10, -10, 5, -5, 0])
    if k % 512:
        return np.exp2(np.random.permutation(np.resize(levels, k // 32))).repeat(32)
    a = np.empty((k // 512, 16))
    for p in range(k // 512):
        a[p, :8] = np.random.permutation(np.resize(levels, 8))
        for g in range(8):
            far = levels[np.abs(levels - a[p, g]) >= 10]
            a[p, g + 8] = far[np.random.randint(len(far))]
    return np.exp2(a.ravel()).repeat(32)


def f64(x):
    return np.asarray(x).astype(np.float64)


def striped(idx):
    return np.tile(idx.reshape(-1, 16).T, (8, 1)).astype(np.uint16)


def unstriped(offs):
    return offs[:16].T.reshape(-1).astype(np.int64)


def striped8(idx):
    return np.concatenate([x.reshape(-1, 16).T for x in idx]).astype(np.uint16)


def runs(offs, k):
    lists = np.stack([offs[16 * r : 16 * r + 16].T.reshape(-1) for r in range(8)]).astype(np.int64)
    return lists[np.arange(k) % 512 // 64]


def pack_weight(w):
    k, n = w.shape
    w = f64(np.asarray(w, np.float32).astype(ml_dtypes.bfloat16)).reshape(k // 32, 32, n)
    amax = np.abs(w).max(1)
    byte = np.clip(np.where(amax > 0, np.frexp(amax)[1] - 1 + 127 - 7, 1), 1, 254)
    scaled = (w * np.exp2(127.0 - byte)[:, None, :]).reshape(k, n).astype(np.float32)
    words = np.ascontiguousarray(scaled.reshape(k // 512, 128, 4, n).transpose(0, 1, 3, 2)).astype(ml_dtypes.float8_e4m3fn).view(np.uint8)
    return words, np.ascontiguousarray(byte.astype(np.uint8).reshape(k // 512, 16, n))


def unpack_weight(words, scales):
    g, p, n, _ = words.shape
    vals = np.ascontiguousarray(words).view(ml_dtypes.float8_e4m3fn).astype(np.float64) * np.repeat(np.exp2(scales.astype(np.float64) - 127.0), 8, axis=1)[..., None]
    return vals.transpose(0, 1, 3, 2).reshape(g * 512, n)


def relu(v):
    return np.maximum(v, 0.0)


def sigmoid(v):
    return 1.0 / (1.0 + np.exp(-np.maximum(v, -700.0)))


K, T, S, G, H, C, W = 512, 1024, 512, 2048, 512, 512, 256


def setup_inputs():
    n = np.random.standard_normal
    s = mx_kscale(K)[:, None]
    packed_xT = pack_weight(n((K, T)) * s)
    packed_dT = pack_weight(n((K, G)) / s)
    perm = np.stack([np.random.permutation(S) for _ in range(8)])
    return {
        "x_words": packed_xT[0],
        "x_scales": packed_xT[1],
        "d_words": packed_dT[0],
        "d_scales": packed_dT[1],
        "gs": (np.random.uniform(0.5, 1.5, (K, 1)) / s).astype(np.float32),
        "offs": striped(np.random.permutation(T)[:S]),
        "k1": striped8(np.random.randint(0, G, (8, H))),
        "n1": striped8(np.stack([np.random.permutation(S) for _ in range(8)])),
        "n2": striped8(np.stack([np.random.permutation(S) for _ in range(8)])),
        "cand": striped(np.random.permutation(T)[:C]),
        "n3": striped8(perm[:, :W]),
        "n4": striped8(perm[:, W:]),
    }


def reference(x_words, x_scales, d_words, d_scales, gs, offs, k1, n1, n2, cand, n3, n4):
    x_cand = unpack_weight(x_words, x_scales)[:, unstriped(cand)]
    d_k1 = unpack_weight(d_words, d_scales)[np.arange(K)[:, None], runs(k1, K)]
    xq = unpack_weight(x_words, x_scales)[:, unstriped(offs)]
    h = 0.0625 * (d_k1.T @ xq)
    pa = h - (h[np.arange(H)[:, None], runs(n1, H)])
    pb = h[np.arange(H)[:, None], runs(n2, H)] - h
    z = f64(gs) * (relu(np.minimum(pa, pb)) - (relu(-1.0 * np.maximum(pa, pb))))
    s = 0.0625 * ((x_cand.T @ mxq(z, 0, "e4m3")))
    pa2 = s[np.arange(C)[:, None], runs(n3, C)]
    pb2 = s[np.arange(C)[:, None], runs(n4, C)]
    ra = pa2 * sigmoid(pb2)
    out = s.copy()
    out[np.arange(C)[:, None], runs(n4, C)] = ra
    return out

@@ -1,0 +1,190 @@
+from contextlib import ExitStack
+
+import concourse.mybir as mybir
+
+K, T, S, G, H, C, W = 512, 1024, 512, 2048, 512, 512, 256
+FLOPS = 2 * K * H * S + 2 * K * C * S
+
+F32 = mybir.dt.float32
+BF16 = mybir.dt.bfloat16
+I32 = mybir.dt.int32
+U32 = mybir.dt.uint32
+U16 = mybir.dt.uint16
+U8 = mybir.dt.uint8
+FP8X4 = mybir.dt.float8_e4m3fn_x4
+ALU = mybir.AluOpType
+ACT = mybir.ActivationFunctionType
+
+P = 128
+PACK = 4
+SIXTEENTH = 0.0625
+CHUNKS = ((0, 256), (256, 128), (384, 128))
+
+
+def tile_picked_pqcminmodfold_none_p_kernel(
+    tc, x_words, x_scales, d_words, d_scales, gs, offs, k1, n1, n2, cand, n3, n4, out
+):
+    nc = tc.nc
+    with ExitStack() as ctx:
+        lists = ctx.enter_context(tc.tile_pool(name="lists", bufs=1))
+        keep = ctx.enter_context(tc.tile_pool(name="keep", bufs=1))
+        psum = ctx.enter_context(tc.psum_pool(name="psum", bufs=1))
+
+        def load_list(name, src):
+            tile = lists.tile(list(src.shape), U16, name=name)
+            nc.sync.dma_start(tile[:], src)
+            return tile
+
+        warm = keep.tile([P, 8], F32, name="warm")
+        warm_out = keep.tile([P, 8], F32, name="warm_out")
+        nc.gpsimd.memset(warm[:], 0.0)
+        nc.scalar.activation(warm_out[:], warm[:], ACT.Sigmoid)
+
+        d_bytes = keep.tile([P, G], U8, name="d_bytes", align_bytes=64)
+        x_bytes = keep.tile([P, T], U8, name="x_bytes", align_bytes=64)
+        nc.vector.memset(d_bytes[:].bitcast(I32), 0)
+        nc.vector.memset(x_bytes[:].bitcast(I32), 0)
+
+        k1_t = load_list("k1_t", k1)
+        for e in range(2):
+            nc.sync.dma_start(d_bytes[e:P:16, :].bitcast(I32), d_scales[0, e:16:2, :].bitcast(I32))
+        offs_t = load_list("offs_t", offs)
+        for q in range(4):
+            queue = nc.sync
+            queue.dma_start(x_bytes[32 * q : 32 * q + 4, :].bitcast(I32), x_scales[0, 4 * q : 4 * q + 4, :].bitcast(I32))
+        d_tab = keep.tile([P, G], U32, name="d_tab", align_bytes=64)
+        x_tab = keep.tile([P, T], U32, name="x_tab", align_bytes=64)
+        nc.sync.dma_start(d_tab[:].bitcast(I32), d_words[0].rearrange("p n t -> p (n t)").bitcast(I32))
+        nc.sync.dma_start(x_tab[:].bitcast(I32), x_words[0].rearrange("p n t -> p (n t)").bitcast(I32))
+        gain = keep.tile([P, PACK], F32, name="gain")
+        nc.gpsimd.dma_start(gain[:], gs.rearrange("(p t) o -> p (t o)", t=PACK))
+        cand_t = load_list("cand_t", cand)
+        n1_t = load_list("n1_t", n1)
+        n2_t = load_list("n2_t", n2)
+        n3_t = load_list("n3_t", n3)
+        n4_t = load_list("n4_t", n4)
+
+        db_pick = keep.tile([P, H], U8, name="db_pick", align_bytes=64)
+        db_dealt = keep.tile([P, H], U8, name="db_dealt", align_bytes=64)
+        nc.vector.tensor_copy(db_pick[:], d_bytes[:].indirect(k1_t[:]))
+        nc.vector.tensor_copy(
+            db_dealt[:].rearrange("p (t m) -> p m t", t=PACK), db_pick[:].rearrange("p (m t) -> p m t", t=PACK)
+        )
+        for e in range(2):
+            nc.scalar.dma_start(db_dealt[2 + e : P : 32, :].bitcast(I32), db_dealt[16 + e : P : 32, :].bitcast(I32))
+
+        dw_pick = keep.tile([P, H], U32, name="dw_pick", align_bytes=64)
+        dw_dealt = keep.tile([P, H], U32, name="dw_dealt", align_bytes=64)
+        nc.vector.tensor_copy(dw_pick[:], d_tab[:].indirect(k1_t[:]))
+        nc.vector.tensor_copy(
+            dw_dealt[:].rearrange("p (t m) -> p m t", t=PACK), dw_pick[:].rearrange("p (m t) -> p m t", t=PACK)
+        )
+        xb_pick = keep.tile([P, S], U8, name="xb_pick", align_bytes=64)
+        xw_pick = keep.tile([P, S], U32, name="xw_pick", align_bytes=64)
+        nc.vector.tensor_copy(xb_pick[:], x_bytes[:].indirect(offs_t[:]))
+        nc.vector.tensor_copy(xw_pick[:], x_tab[:].indirect(offs_t[:]))
+
+        h_win, h_own = [], []
+        for t in range(PACK):
+            bank = psum.tile([P, S], F32, name=f"h_bank{t}")
+            cols = slice(t * P, (t + 1) * P)
+            nc.tensor.matmul_mx(
+                out=bank[:],
+                lhsT=dw_dealt[:, cols].bitcast(FP8X4),
+                lhsT_scale=db_dealt[:, cols],
+                rhs=xw_pick[:].bitcast(FP8X4),
+                rhs_scale=xb_pick[:],
+                start=True,
+                stop=True,
+            )
+            win = keep.tile([P, S], F32, name=f"h_win{t}", align_bytes=64)
+            own = keep.tile([P, S], F32, name=f"h_own{t}", align_bytes=64)
+            nc.scalar.activation(win[:], bank[:], ACT.Copy, scale=gain[:, t : t + 1])
+            nc.scalar.activation(own[:], bank[:], ACT.Copy, scale=gain[:, t : t + 1])
+            h_win.append(win)
+            h_own.append(own)
+
+        cw_dealt = keep.tile([P, C], U32, name="cw_dealt", align_bytes=64)
+        cb_pick = keep.tile([P, C], U8, name="cb_pick", align_bytes=64)
+        cb_dealt = keep.tile([P, C], U8, name="cb_dealt", align_bytes=64)
+        nc.vector.tensor_copy(
+            cw_dealt[:].rearrange("p (t g e) -> p g t e", t=PACK, e=8), x_tab[:].indirect(cand_t[:])
+        )
+        nc.vector.tensor_copy(cb_pick[:], x_bytes[:].indirect(cand_t[:]))
+        nc.vector.tensor_copy(
+            cb_dealt[:].bitcast(I32).rearrange("p (t g e) -> p g t e", t=PACK, e=2),
+            cb_pick[:].bitcast(I32).rearrange("p (g t e) -> p g t e", t=PACK, e=2),
+        )
+
+        s_banks = [psum.tile([P, S], F32, name=f"s_bank{t}") for t in range(PACK)]
+        s_rows = [keep.tile([P, S], F32, name=f"s_rows{t}", align_bytes=64) for t in range(PACK)]
+
+        def fetch(c):
+            first, width = CHUNKS[c]
+            cols = slice(first, first + width)
+            entries = slice(first // 16, (first + width) // 16)
+            diffs = []
+            for name, lst in (("na", n1_t), ("pb", n2_t)):
+                diff = keep.tile([P, PACK, width], F32, name=f"{name}{c}", align_bytes=64)
+                for t in range(PACK):
+                    nc.vector.tensor_tensor(
+                        diff[:, t, :], h_win[t][:].indirect(lst[:, entries]), h_own[t][:, cols], ALU.subtract
+                    )
+                diffs.append(diff)
+            woven = []
+            for name, diff, func, scale in (
+                ("pa16", diffs[0], ACT.Copy, -SIXTEENTH),
+                ("hi16", diffs[0], ACT.Relu, -SIXTEENTH),
+                ("pb16", diffs[1], ACT.Copy, SIXTEENTH),
+            ):
+                dst = keep.tile([P, width, PACK], BF16, name=f"{name}_{c}", align_bytes=64)
+                nc.scalar.activation(
+                    dst[:].rearrange("p (c i) t -> p c t i", i=4),
+                    diff[:].rearrange("p t (c i) -> p c t i", i=4),
+                    func,
+                    scale=scale,
+                )
+                woven.append(dst[:].rearrange("p j t -> p (j t)"))
+            return woven
+
+        def score(c, woven):
+            first, width = CHUNKS[c]
+            cols = slice(first, first + width)
+            pa16, hi16, pb16 = woven
+            lo16 = keep.tile([P, width * PACK], BF16, name=f"lo16_{c}", align_bytes=64)
+            mid16 = keep.tile([P, width * PACK], BF16, name=f"mid16_{c}", align_bytes=64)
+            z16 = keep.tile([P, width * PACK], BF16, name=f"z16_{c}", align_bytes=64)
+            nc.vector.tensor_scalar_min(lo16[:], pa16, 0.0)
+            nc.vector.tensor_tensor(mid16[:], pb16, lo16[:], ALU.max)
+            nc.vector.tensor_tensor(z16[:], mid16[:], hi16, ALU.min)
+            z_words = keep.tile([P, width], U32, name=f"z_words{c}", align_bytes=64)
+            z_bytes = keep.tile([P, width], U8, name=f"z_bytes{c}", align_bytes=64)
+            nc.vector.quantize_mx(out=z_words[:].bitcast(FP8X4), scales=z_bytes[:], in_=z16[:])
+            for t in range(PACK):
+                rows = slice(t * P, (t + 1) * P)
+                nc.tensor.matmul_mx(
+                    out=s_banks[t][:, cols],
+                    lhsT=cw_dealt[:, rows].bitcast(FP8X4),
+                    lhsT_scale=cb_dealt[:, rows],
+                    rhs=z_words[:].bitcast(FP8X4),
+                    rhs_scale=z_bytes[:],
+                    start=True,
+                    stop=True,
+                )
+                nc.scalar.activation(s_rows[t][:, cols], s_banks[t][:, cols], ACT.Copy, scale=SIXTEENTH)
+
+        woven = fetch(0)
+        for c in range(1, len(CHUNKS)):
+            ahead = fetch(c)
+            score(c - 1, woven)
+            woven = ahead
+        score(len(CHUNKS) - 1, woven)
+
+        out_rows = out.rearrange("(g t e) j -> t g e j", t=PACK, e=8)
+        for t in range(PACK):
+            pa2 = keep.tile([P, W], F32, name=f"pa2_{t}", align_bytes=64)
+            gate = keep.tile([P, W], F32, name=f"gate{t}", align_bytes=64)
+            nc.vector.tensor_copy(pa2[:], s_rows[t][:].indirect(n3_t[:]))
+            nc.scalar.activation(gate[:], s_rows[t][:].indirect(n4_t[:]), ACT.Sigmoid)
+            nc.vector.tensor_tensor(s_rows[t][:].indirect(n4_t[:]), pa2[:], gate[:], ALU.mult)
+            nc.sync.dma_start(out_rows[t], s_rows[t][:])

@@ -18,7 +18,6 @@ ACT = mybir.ActivationFunctionType
 P = 128
 PACK = 4
 SIXTEENTH = 0.0625
-CHUNKS = ((0, 256), (256, 128), (384, 128))
 
 
 def tile_picked_pqcminmodfold_none_p_kernel(
@@ -42,23 +41,20 @@ def tile_picked_pqcminmodfold_none_p_kernel(
 
         d_bytes = keep.tile([P, G], U8, name="d_bytes", align_bytes=64)
         x_bytes = keep.tile([P, T], U8, name="x_bytes", align_bytes=64)
-        nc.vector.memset(d_bytes[:].bitcast(I32), 0)
         nc.vector.memset(x_bytes[:].bitcast(I32), 0)
 
         k1_t = load_list("k1_t", k1)
-        for e in range(2):
-            nc.sync.dma_start(d_bytes[e:P:16, :].bitcast(I32), d_scales[0, e:16:2, :].bitcast(I32))
+        nc.sync.dma_start(d_bytes[:].bitcast(I32), d_scales[0].bitcast(I32).unsqueeze(1).broadcast_to([16, 8, G // 4]))
         offs_t = load_list("offs_t", offs)
-        for q in range(4):
-            queue = nc.sync
-            queue.dma_start(x_bytes[32 * q : 32 * q + 4, :].bitcast(I32), x_scales[0, 4 * q : 4 * q + 4, :].bitcast(I32))
         d_tab = keep.tile([P, G], U32, name="d_tab", align_bytes=64)
         x_tab = keep.tile([P, T], U32, name="x_tab", align_bytes=64)
-        nc.sync.dma_start(d_tab[:].bitcast(I32), d_words[0].rearrange("p n t -> p (n t)").bitcast(I32))
         nc.sync.dma_start(x_tab[:].bitcast(I32), x_words[0].rearrange("p n t -> p (n t)").bitcast(I32))
+        nc.sync.dma_start(d_tab[:].bitcast(I32), d_words[0].rearrange("p n t -> p (n t)").bitcast(I32))
+        for q in range(4):
+            nc.sync.dma_start(x_bytes[32 * q : 32 * q + 4, :].bitcast(I32), x_scales[0, 4 * q : 4 * q + 4, :].bitcast(I32))
+        cand_t = load_list("cand_t", cand)
         gain = keep.tile([P, PACK], F32, name="gain")
         nc.gpsimd.dma_start(gain[:], gs.rearrange("(p t) o -> p (t o)", t=PACK))
-        cand_t = load_list("cand_t", cand)
         n1_t = load_list("n1_t", n1)
         n2_t = load_list("n2_t", n2)
         n3_t = load_list("n3_t", n3)
@@ -70,23 +66,27 @@ def tile_picked_pqcminmodfold_none_p_kernel(
         nc.vector.tensor_copy(
             db_dealt[:].rearrange("p (t m) -> p m t", t=PACK), db_pick[:].rearrange("p (m t) -> p m t", t=PACK)
         )
-        for e in range(2):
-            nc.scalar.dma_start(db_dealt[2 + e : P : 32, :].bitcast(I32), db_dealt[16 + e : P : 32, :].bitcast(I32))
+        for j in range(1, 4):
+            nc.scalar.dma_start(db_dealt[j:P:32, :].bitcast(I32), db_dealt[8 * j : P : 32, :].bitcast(I32))
 
-        dw_pick = keep.tile([P, H], U32, name="dw_pick", align_bytes=64)
-        dw_dealt = keep.tile([P, H], U32, name="dw_dealt", align_bytes=64)
-        nc.vector.tensor_copy(dw_pick[:], d_tab[:].indirect(k1_t[:]))
-        nc.vector.tensor_copy(
-            dw_dealt[:].rearrange("p (t m) -> p m t", t=PACK), dw_pick[:].rearrange("p (m t) -> p m t", t=PACK)
-        )
         xb_pick = keep.tile([P, S], U8, name="xb_pick", align_bytes=64)
         xw_pick = keep.tile([P, S], U32, name="xw_pick", align_bytes=64)
-        nc.vector.tensor_copy(xb_pick[:], x_bytes[:].indirect(offs_t[:]))
         nc.vector.tensor_copy(xw_pick[:], x_tab[:].indirect(offs_t[:]))
+        dw_dealt = keep.tile([P, H], U32, name="dw_dealt", align_bytes=64)
+        dw_pick = [keep.tile([P, H // 2], U32, name=f"dw_pick{u}", tag=f"stage{u}", align_bytes=64) for u in range(2)]
+        for u in range(2):
+            nc.vector.tensor_copy(dw_pick[u][:], d_tab[:].indirect(k1_t[:, 16 * u : 16 * (u + 1)]))
+        nc.vector.tensor_copy(xb_pick[:], x_bytes[:].indirect(offs_t[:]))
+        for u in range(2):
+            nc.vector.tensor_copy(
+                dw_dealt[:].rearrange("p (t m) -> p m t", t=PACK)[:, 64 * u : 64 * (u + 1), :],
+                dw_pick[u][:].rearrange("p (m t) -> p m t", t=PACK),
+            )
 
-        h_win, h_own = [], []
+        half = S // 2
+        h_banks, h_win, h_own = [], [], []
         for t in range(PACK):
-            bank = psum.tile([P, S], F32, name=f"h_bank{t}")
+            bank = psum.tile([P, S], F32, name=f"h_bank{t}", tag=f"bank{t}")
             cols = slice(t * P, (t + 1) * P)
             nc.tensor.matmul_mx(
                 out=bank[:],
@@ -100,12 +100,15 @@ def tile_picked_pqcminmodfold_none_p_kernel(
             win = keep.tile([P, S], F32, name=f"h_win{t}", align_bytes=64)
             own = keep.tile([P, S], F32, name=f"h_own{t}", align_bytes=64)
             nc.scalar.activation(win[:], bank[:], ACT.Copy, scale=gain[:, t : t + 1])
-            nc.scalar.activation(own[:], bank[:], ACT.Copy, scale=gain[:, t : t + 1])
+            nc.scalar.activation(own[:, :half], bank[:, :half], ACT.Copy, scale=gain[:, t : t + 1])
+            h_banks.append(bank)
             h_win.append(win)
             h_own.append(own)
+        for t in range(PACK):
+            nc.scalar.activation(h_own[t][:, half:], h_banks[t][:, half:], ACT.Copy, scale=gain[:, t : t + 1])
 
-        cw_dealt = keep.tile([P, C], U32, name="cw_dealt", align_bytes=64)
-        cb_pick = keep.tile([P, C], U8, name="cb_pick", align_bytes=64)
+        cw_dealt = keep.tile([P, C], U32, name="cw_dealt", tag="stage0", align_bytes=64)
+        cb_pick = keep.tile([P, C], U8, name="cb_pick", tag="stage1", align_bytes=64)
         cb_dealt = keep.tile([P, C], U8, name="cb_dealt", align_bytes=64)
         nc.vector.tensor_copy(
             cw_dealt[:].rearrange("p (t g e) -> p g t e", t=PACK, e=8), x_tab[:].indirect(cand_t[:])
@@ -116,54 +119,49 @@ def tile_picked_pqcminmodfold_none_p_kernel(
             cb_pick[:].bitcast(I32).rearrange("p (g t e) -> p g t e", t=PACK, e=2),
         )
 
-        s_banks = [psum.tile([P, S], F32, name=f"s_bank{t}") for t in range(PACK)]
+        s_banks = [
+            [psum.tile([P, half], F32, name=f"s_bank{c}_{t}", tag=f"bank{(PACK * (c + 1) + t) % (2 * PACK)}") for t in range(PACK)]
+            for c in range(2)
+        ]
         s_rows = [keep.tile([P, S], F32, name=f"s_rows{t}", align_bytes=64) for t in range(PACK)]
 
-        def fetch(c):
-            first, width = CHUNKS[c]
-            cols = slice(first, first + width)
-            entries = slice(first // 16, (first + width) // 16)
-            diffs = []
-            for name, lst in (("na", n1_t), ("pb", n2_t)):
-                diff = keep.tile([P, PACK, width], F32, name=f"{name}{c}", align_bytes=64)
-                for t in range(PACK):
-                    nc.vector.tensor_tensor(
-                        diff[:, t, :], h_win[t][:].indirect(lst[:, entries]), h_own[t][:, cols], ALU.subtract
-                    )
-                diffs.append(diff)
-            woven = []
-            for name, diff, func, scale in (
-                ("pa16", diffs[0], ACT.Copy, -SIXTEENTH),
-                ("hi16", diffs[0], ACT.Relu, -SIXTEENTH),
-                ("pb16", diffs[1], ACT.Copy, SIXTEENTH),
-            ):
-                dst = keep.tile([P, width, PACK], BF16, name=f"{name}_{c}", align_bytes=64)
-                nc.scalar.activation(
-                    dst[:].rearrange("p (c i) t -> p c t i", i=4),
-                    diff[:].rearrange("p t (c i) -> p c t i", i=4),
-                    func,
-                    scale=scale,
-                )
-                woven.append(dst[:].rearrange("p j t -> p (j t)"))
-            return woven
+        def difference(diff, lst, c, t):
+            cols = slice(c * half, (c + 1) * half)
+            entries = slice(c * half // 16, (c + 1) * half // 16)
+            nc.vector.tensor_tensor(diff[:, t, :], h_win[t][:].indirect(lst[:, entries]), h_own[t][:, cols], ALU.subtract)
 
-        def score(c, woven):
-            first, width = CHUNKS[c]
-            cols = slice(first, first + width)
-            pa16, hi16, pb16 = woven
-            lo16 = keep.tile([P, width * PACK], BF16, name=f"lo16_{c}", align_bytes=64)
-            mid16 = keep.tile([P, width * PACK], BF16, name=f"mid16_{c}", align_bytes=64)
-            z16 = keep.tile([P, width * PACK], BF16, name=f"z16_{c}", align_bytes=64)
-            nc.vector.tensor_scalar_min(lo16[:], pa16, 0.0)
-            nc.vector.tensor_tensor(mid16[:], pb16, lo16[:], ALU.max)
-            nc.vector.tensor_tensor(z16[:], mid16[:], hi16, ALU.min)
-            z_words = keep.tile([P, width], U32, name=f"z_words{c}", align_bytes=64)
-            z_bytes = keep.tile([P, width], U8, name=f"z_bytes{c}", align_bytes=64)
-            nc.vector.quantize_mx(out=z_words[:].bitcast(FP8X4), scales=z_bytes[:], in_=z16[:])
+        def weave(name, diff, cols, func, scale):
+            width = cols.stop - cols.start
+            dst = keep.tile([P, width, PACK], BF16, name=name, align_bytes=64)
+            nc.scalar.activation(
+                dst[:].rearrange("p (c i) t -> p c t i", i=4),
+                diff[:, :, cols].rearrange("p t (c i) -> p c t i", i=4),
+                func,
+                scale=scale,
+            )
+            return dst[:].rearrange("p j t -> p (j t)")
+
+        def combine(name, a, b, op):
+            dst = keep.tile(list(a.shape), BF16, name=name, align_bytes=64)
+            nc.vector.tensor_tensor(dst[:], a, b, op)
+            return dst[:]
+
+        def lower(name, pa16):
+            dst = keep.tile(list(pa16.shape), BF16, name=name, align_bytes=64)
+            nc.vector.tensor_scalar_min(dst[:], pa16, 0.0)
+            return dst[:]
+
+        def score(first, z16):
+            width = z16.shape[1] // PACK
+            c = first // half
+            cols = slice(first % half, first % half + width)
+            z_words = keep.tile([P, width], U32, name=f"z_words{first}", align_bytes=64)
+            z_bytes = keep.tile([P, width], U8, name=f"z_bytes{first}", align_bytes=64)
+            nc.vector.quantize_mx(out=z_words[:].bitcast(FP8X4), scales=z_bytes[:], in_=z16)
             for t in range(PACK):
                 rows = slice(t * P, (t + 1) * P)
                 nc.tensor.matmul_mx(
-                    out=s_banks[t][:, cols],
+                    out=s_banks[c][t][:, cols],
                     lhsT=cw_dealt[:, rows].bitcast(FP8X4),
                     lhsT_scale=cb_dealt[:, rows],
                     rhs=z_words[:].bitcast(FP8X4),
@@ -171,20 +169,58 @@ def tile_picked_pqcminmodfold_none_p_kernel(
                     start=True,
                     stop=True,
                 )
-                nc.scalar.activation(s_rows[t][:, cols], s_banks[t][:, cols], ACT.Copy, scale=SIXTEENTH)
 
-        woven = fetch(0)
-        for c in range(1, len(CHUNKS)):
-            ahead = fetch(c)
-            score(c - 1, woven)
-            woven = ahead
-        score(len(CHUNKS) - 1, woven)
+        def empty(c, t):
+            nc.scalar.activation(s_rows[t][:, c * half : (c + 1) * half], s_banks[c][t][:], ACT.Copy, scale=SIXTEENTH)
+
+        whole = slice(0, half)
+        na0 = keep.tile([P, PACK, half], F32, name="na0", align_bytes=64)
+        pb0 = keep.tile([P, PACK, half], F32, name="pb0", tag="pb", align_bytes=64)
+        for t in range(PACK):
+            difference(na0, n1_t, 0, t)
+            difference(pb0, n2_t, 0, t)
+        pa16_0 = weave("pa16_0", na0, whole, ACT.Copy, -SIXTEENTH)
+        pb16_0 = weave("pb16_0", pb0, whole, ACT.Copy, SIXTEENTH)
+        hi16_0 = weave("hi16_0", na0, whole, ACT.Relu, -SIXTEENTH)
+        na1 = keep.tile([P, PACK, half], F32, name="na1", align_bytes=64)
+        for t in range(PACK):
+            difference(na1, n1_t, 1, t)
+        pa16_1 = weave("pa16_1", na1, whole, ACT.Copy, -SIXTEENTH)
+        hi16_1 = weave("hi16_1", na1, whole, ACT.Relu, -SIXTEENTH)
+        lo16_0 = lower("lo16_0", pa16_0)
+        pb1 = keep.tile([P, PACK, half], F32, name="pb1", tag="pb", align_bytes=64)
+        difference(pb1, n2_t, 1, 0)
+        mid16_0 = combine("mid16_0", pb16_0, lo16_0, ALU.max)
+        for t in range(1, PACK):
+            difference(pb1, n2_t, 1, t)
+        quarter = half // 2
+        pb16_1 = [weave(f"pb16_1{u}", pb1, slice(u * quarter, (u + 1) * quarter), ACT.Copy, SIXTEENTH) for u in range(2)]
+        z16_0 = combine("z16_0", mid16_0, hi16_0, ALU.min)
+        lo16_1 = lower("lo16_1", pa16_1)
+        score(0, z16_0)
+        for t in range(PACK):
+            empty(0, t)
+        parts = [slice(u * quarter * PACK, (u + 1) * quarter * PACK) for u in range(2)]
+        mid16_1 = [combine(f"mid16_1{u}", pb16_1[u], lo16_1[:, parts[u]], ALU.max) for u in range(2)]
+        z16_1 = [combine(f"z16_1{u}", mid16_1[u], hi16_1[:, parts[u]], ALU.min) for u in range(2)]
+        for u in range(2):
+            score(half + u * quarter, z16_1[u])
 
         out_rows = out.rearrange("(g t e) j -> t g e j", t=PACK, e=8)
+        pa2 = [keep.tile([P, W], F32, name=f"pa2_{t}", align_bytes=64) for t in range(PACK)]
+        gate = [keep.tile([P, W], F32, name=f"gate{t}", align_bytes=64) for t in range(PACK)]
+
+        def fetch_pair(t):
+            nc.scalar.activation(gate[t][:], s_rows[t][:].indirect(n4_t[:]), ACT.Sigmoid)
+            nc.vector.tensor_copy(pa2[t][:], s_rows[t][:].indirect(n3_t[:]))
+
+        empty(1, 0)
+        empty(1, 1)
+        fetch_pair(0)
         for t in range(PACK):
-            pa2 = keep.tile([P, W], F32, name=f"pa2_{t}", align_bytes=64)
-            gate = keep.tile([P, W], F32, name=f"gate{t}", align_bytes=64)
-            nc.vector.tensor_copy(pa2[:], s_rows[t][:].indirect(n3_t[:]))
-            nc.scalar.activation(gate[:], s_rows[t][:].indirect(n4_t[:]), ACT.Sigmoid)
-            nc.vector.tensor_tensor(s_rows[t][:].indirect(n4_t[:]), pa2[:], gate[:], ALU.mult)
+            if t + 2 < PACK:
+                empty(1, t + 2)
+            if t + 1 < PACK:
+                fetch_pair(t + 1)
+            nc.vector.tensor_tensor(s_rows[t][:].indirect(n4_t[:]), pa2[t][:], gate[t][:], ALU.mult)
             nc.sync.dma_start(out_rows[t], s_rows[t][:])

@@ -49,9 +49,9 @@ def tile_picked_pqcminmodfold_none_p_kernel(
         d_tab = keep.tile([P, G], U32, name="d_tab", align_bytes=64)
         x_tab = keep.tile([P, T], U32, name="x_tab", align_bytes=64)
         nc.sync.dma_start(x_tab[:].bitcast(I32), x_words[0].rearrange("p n t -> p (n t)").bitcast(I32))
-        nc.sync.dma_start(d_tab[:].bitcast(I32), d_words[0].rearrange("p n t -> p (n t)").bitcast(I32))
         for q in range(4):
             nc.sync.dma_start(x_bytes[32 * q : 32 * q + 4, :].bitcast(I32), x_scales[0, 4 * q : 4 * q + 4, :].bitcast(I32))
+        nc.sync.dma_start(d_tab[:].bitcast(I32), d_words[0].rearrange("p n t -> p (n t)").bitcast(I32))
         cand_t = load_list("cand_t", cand)
         gain = keep.tile([P, PACK], F32, name="gain")
         nc.gpsimd.dma_start(gain[:], gs.rearrange("(p t) o -> p (t o)", t=PACK))
@@ -72,11 +72,11 @@ def tile_picked_pqcminmodfold_none_p_kernel(
         xb_pick = keep.tile([P, S], U8, name="xb_pick", align_bytes=64)
         xw_pick = keep.tile([P, S], U32, name="xw_pick", align_bytes=64)
         nc.vector.tensor_copy(xw_pick[:], x_tab[:].indirect(offs_t[:]))
+        nc.vector.tensor_copy(xb_pick[:], x_bytes[:].indirect(offs_t[:]))
         dw_dealt = keep.tile([P, H], U32, name="dw_dealt", align_bytes=64)
         dw_pick = [keep.tile([P, H // 2], U32, name=f"dw_pick{u}", tag=f"stage{u}", align_bytes=64) for u in range(2)]
         for u in range(2):
             nc.vector.tensor_copy(dw_pick[u][:], d_tab[:].indirect(k1_t[:, 16 * u : 16 * (u + 1)]))
-        nc.vector.tensor_copy(xb_pick[:], x_bytes[:].indirect(offs_t[:]))
         for u in range(2):
             nc.vector.tensor_copy(
                 dw_dealt[:].rearrange("p (t m) -> p m t", t=PACK)[:, 64 * u : 64 * (u + 1), :],
@@ -107,13 +107,13 @@ def tile_picked_pqcminmodfold_none_p_kernel(
         for t in range(PACK):
             nc.scalar.activation(h_own[t][:, half:], h_banks[t][:, half:], ACT.Copy, scale=gain[:, t : t + 1])
 
-        cw_dealt = keep.tile([P, C], U32, name="cw_dealt", tag="stage0", align_bytes=64)
-        cb_pick = keep.tile([P, C], U8, name="cb_pick", tag="stage1", align_bytes=64)
+        cw_dealt = keep.tile([P, C], U32, name="cw_dealt", tag="stage1", align_bytes=64)
+        cb_pick = keep.tile([P, C], U8, name="cb_pick", tag="stage0", align_bytes=64)
         cb_dealt = keep.tile([P, C], U8, name="cb_dealt", align_bytes=64)
+        nc.vector.tensor_copy(cb_pick[:], x_bytes[:].indirect(cand_t[:]))
         nc.vector.tensor_copy(
             cw_dealt[:].rearrange("p (t g e) -> p g t e", t=PACK, e=8), x_tab[:].indirect(cand_t[:])
         )
-        nc.vector.tensor_copy(cb_pick[:], x_bytes[:].indirect(cand_t[:]))
         nc.vector.tensor_copy(
             cb_dealt[:].bitcast(I32).rearrange("p (t g e) -> p g t e", t=PACK, e=2),
             cb_pick[:].bitcast(I32).rearrange("p (g t e) -> p g t e", t=PACK, e=2),

@@ -41,10 +41,11 @@ def tile_picked_pqcminmodfold_none_p_kernel(
 
         d_bytes = keep.tile([P, G], U8, name="d_bytes", align_bytes=64)
         x_bytes = keep.tile([P, T], U8, name="x_bytes", align_bytes=64)
+        nc.vector.memset(d_bytes[:].bitcast(I32), 0)
         nc.vector.memset(x_bytes[:].bitcast(I32), 0)
 
         k1_t = load_list("k1_t", k1)
-        nc.sync.dma_start(d_bytes[:].bitcast(I32), d_scales[0].bitcast(I32).unsqueeze(1).broadcast_to([16, 8, G // 4]))
+        nc.sync.dma_start(d_bytes[0:P:8, :].bitcast(I32), d_scales[0].bitcast(I32))
         offs_t = load_list("offs_t", offs)
         d_tab = keep.tile([P, G], U32, name="d_tab", align_bytes=64)
         x_tab = keep.tile([P, T], U32, name="x_tab", align_bytes=64)

from contextlib import ExitStack

import concourse.mybir as mybir

K, T, S, G, H, C, W = 512, 1024, 512, 2048, 512, 512, 256
FLOPS = 2 * K * H * S + 2 * K * C * S

F32 = mybir.dt.float32
BF16 = mybir.dt.bfloat16
I32 = mybir.dt.int32
U32 = mybir.dt.uint32
U16 = mybir.dt.uint16
U8 = mybir.dt.uint8
FP8X4 = mybir.dt.float8_e4m3fn_x4
ALU = mybir.AluOpType
ACT = mybir.ActivationFunctionType

P = 128
PACK = 4
SIXTEENTH = 0.0625


def tile_picked_pqcminmodfold_none_p_kernel(
    tc, x_words, x_scales, d_words, d_scales, gs, offs, k1, n1, n2, cand, n3, n4, out
):
    nc = tc.nc
    with ExitStack() as ctx:
        lists = ctx.enter_context(tc.tile_pool(name="lists", bufs=1))
        keep = ctx.enter_context(tc.tile_pool(name="keep", bufs=1))
        psum = ctx.enter_context(tc.psum_pool(name="psum", bufs=1))

        def load_list(name, src):
            tile = lists.tile(list(src.shape), U16, name=name)
            nc.sync.dma_start(tile[:], src)
            return tile

        warm = keep.tile([P, 8], F32, name="warm")
        warm_out = keep.tile([P, 8], F32, name="warm_out")
        nc.gpsimd.memset(warm[:], 0.0)
        nc.scalar.activation(warm_out[:], warm[:], ACT.Sigmoid)

        d_bytes = keep.tile([P, G], U8, name="d_bytes", align_bytes=64)
        x_bytes = keep.tile([P, T], U8, name="x_bytes", align_bytes=64)
        nc.vector.memset(d_bytes[:].bitcast(I32), 0)
        nc.vector.memset(x_bytes[:].bitcast(I32), 0)

        k1_t = load_list("k1_t", k1)
        nc.sync.dma_start(d_bytes[0:P:8, :].bitcast(I32), d_scales[0].bitcast(I32))
        offs_t = load_list("offs_t", offs)
        d_tab = keep.tile([P, G], U32, name="d_tab", align_bytes=64)
        x_tab = keep.tile([P, T], U32, name="x_tab", align_bytes=64)
        nc.sync.dma_start(x_tab[:].bitcast(I32), x_words[0].rearrange("p n t -> p (n t)").bitcast(I32))
        for q in range(4):
            nc.sync.dma_start(x_bytes[32 * q : 32 * q + 4, :].bitcast(I32), x_scales[0, 4 * q : 4 * q + 4, :].bitcast(I32))
        nc.sync.dma_start(d_tab[:].bitcast(I32), d_words[0].rearrange("p n t -> p (n t)").bitcast(I32))
        cand_t = load_list("cand_t", cand)
        gain = keep.tile([P, PACK], F32, name="gain")
        nc.gpsimd.dma_start(gain[:], gs.rearrange("(p t) o -> p (t o)", t=PACK))
        n1_t = load_list("n1_t", n1)
        n2_t = load_list("n2_t", n2)
        n3_t = load_list("n3_t", n3)
        n4_t = load_list("n4_t", n4)

        db_pick = keep.tile([P, H], U8, name="db_pick", align_bytes=64)
        db_dealt = keep.tile([P, H], U8, name="db_dealt", align_bytes=64)
        nc.vector.tensor_copy(db_pick[:], d_bytes[:].indirect(k1_t[:]))
        nc.vector.tensor_copy(
            db_dealt[:].rearrange("p (t m) -> p m t", t=PACK), db_pick[:].rearrange("p (m t) -> p m t", t=PACK)
        )
        for j in range(1, 4):
            nc.scalar.dma_start(db_dealt[j:P:32, :].bitcast(I32), db_dealt[8 * j : P : 32, :].bitcast(I32))

        xb_pick = keep.tile([P, S], U8, name="xb_pick", align_bytes=64)
        xw_pick = keep.tile([P, S], U32, name="xw_pick", align_bytes=64)
        nc.vector.tensor_copy(xw_pick[:], x_tab[:].indirect(offs_t[:]))
        nc.vector.tensor_copy(xb_pick[:], x_bytes[:].indirect(offs_t[:]))
        dw_dealt = keep.tile([P, H], U32, name="dw_dealt", align_bytes=64)
        dw_pick = [keep.tile([P, H // 2], U32, name=f"dw_pick{u}", tag=f"stage{u}", align_bytes=64) for u in range(2)]
        for u in range(2):
            nc.vector.tensor_copy(dw_pick[u][:], d_tab[:].indirect(k1_t[:, 16 * u : 16 * (u + 1)]))
        for u in range(2):
            nc.vector.tensor_copy(
                dw_dealt[:].rearrange("p (t m) -> p m t", t=PACK)[:, 64 * u : 64 * (u + 1), :],
                dw_pick[u][:].rearrange("p (m t) -> p m t", t=PACK),
            )

        half = S // 2
        h_banks, h_win, h_own = [], [], []
        for t in range(PACK):
            bank = psum.tile([P, S], F32, name=f"h_bank{t}", tag=f"bank{t}")
            cols = slice(t * P, (t + 1) * P)
            nc.tensor.matmul_mx(
                out=bank[:],
                lhsT=dw_dealt[:, cols].bitcast(FP8X4),
                lhsT_scale=db_dealt[:, cols],
                rhs=xw_pick[:].bitcast(FP8X4),
                rhs_scale=xb_pick[:],
                start=True,
                stop=True,
            )
            win = keep.tile([P, S], F32, name=f"h_win{t}", align_bytes=64)
            own = keep.tile([P, S], F32, name=f"h_own{t}", align_bytes=64)
            nc.scalar.activation(win[:], bank[:], ACT.Copy, scale=gain[:, t : t + 1])
            nc.scalar.activation(own[:, :half], bank[:, :half], ACT.Copy, scale=gain[:, t : t + 1])
            h_banks.append(bank)
            h_win.append(win)
            h_own.append(own)
        for t in range(PACK):
            nc.scalar.activation(h_own[t][:, half:], h_banks[t][:, half:], ACT.Copy, scale=gain[:, t : t + 1])

        cw_dealt = keep.tile([P, C], U32, name="cw_dealt", tag="stage1", align_bytes=64)
        cb_pick = keep.tile([P, C], U8, name="cb_pick", tag="stage0", align_bytes=64)
        cb_dealt = keep.tile([P, C], U8, name="cb_dealt", align_bytes=64)
        nc.vector.tensor_copy(cb_pick[:], x_bytes[:].indirect(cand_t[:]))
        nc.vector.tensor_copy(
            cw_dealt[:].rearrange("p (t g e) -> p g t e", t=PACK, e=8), x_tab[:].indirect(cand_t[:])
        )
        nc.vector.tensor_copy(
            cb_dealt[:].bitcast(I32).rearrange("p (t g e) -> p g t e", t=PACK, e=2),
            cb_pick[:].bitcast(I32).rearrange("p (g t e) -> p g t e", t=PACK, e=2),
        )

        s_banks = [
            [psum.tile([P, half], F32, name=f"s_bank{c}_{t}", tag=f"bank{(PACK * (c + 1) + t) % (2 * PACK)}") for t in range(PACK)]
            for c in range(2)
        ]
        s_rows = [keep.tile([P, S], F32, name=f"s_rows{t}", align_bytes=64) for t in range(PACK)]

        def difference(diff, lst, c, t):
            cols = slice(c * half, (c + 1) * half)
            entries = slice(c * half // 16, (c + 1) * half // 16)
            nc.vector.tensor_tensor(diff[:, t, :], h_win[t][:].indirect(lst[:, entries]), h_own[t][:, cols], ALU.subtract)

        def weave(name, diff, cols, func, scale):
            width = cols.stop - cols.start
            dst = keep.tile([P, width, PACK], BF16, name=name, align_bytes=64)
            nc.scalar.activation(
                dst[:].rearrange("p (c i) t -> p c t i", i=4),
                diff[:, :, cols].rearrange("p t (c i) -> p c t i", i=4),
                func,
                scale=scale,
            )
            return dst[:].rearrange("p j t -> p (j t)")

        def combine(name, a, b, op):
            dst = keep.tile(list(a.shape), BF16, name=name, align_bytes=64)
            nc.vector.tensor_tensor(dst[:], a, b, op)
            return dst[:]

        def lower(name, pa16):
            dst = keep.tile(list(pa16.shape), BF16, name=name, align_bytes=64)
            nc.vector.tensor_scalar_min(dst[:], pa16, 0.0)
            return dst[:]

        def score(first, z16):
            width = z16.shape[1] // PACK
            c = first // half
            cols = slice(first % half, first % half + width)
            z_words = keep.tile([P, width], U32, name=f"z_words{first}", align_bytes=64)
            z_bytes = keep.tile([P, width], U8, name=f"z_bytes{first}", align_bytes=64)
            nc.vector.quantize_mx(out=z_words[:].bitcast(FP8X4), scales=z_bytes[:], in_=z16)
            for t in range(PACK):
                rows = slice(t * P, (t + 1) * P)
                nc.tensor.matmul_mx(
                    out=s_banks[c][t][:, cols],
                    lhsT=cw_dealt[:, rows].bitcast(FP8X4),
                    lhsT_scale=cb_dealt[:, rows],
                    rhs=z_words[:].bitcast(FP8X4),
                    rhs_scale=z_bytes[:],
                    start=True,
                    stop=True,
                )

        def empty(c, t):
            nc.scalar.activation(s_rows[t][:, c * half : (c + 1) * half], s_banks[c][t][:], ACT.Copy, scale=SIXTEENTH)

        whole = slice(0, half)
        na0 = keep.tile([P, PACK, half], F32, name="na0", align_bytes=64)
        pb0 = keep.tile([P, PACK, half], F32, name="pb0", tag="pb", align_bytes=64)
        for t in range(PACK):
            difference(na0, n1_t, 0, t)
            difference(pb0, n2_t, 0, t)
        pa16_0 = weave("pa16_0", na0, whole, ACT.Copy, -SIXTEENTH)
        pb16_0 = weave("pb16_0", pb0, whole, ACT.Copy, SIXTEENTH)
        hi16_0 = weave("hi16_0", na0, whole, ACT.Relu, -SIXTEENTH)
        na1 = keep.tile([P, PACK, half], F32, name="na1", align_bytes=64)
        for t in range(PACK):
            difference(na1, n1_t, 1, t)
        pa16_1 = weave("pa16_1", na1, whole, ACT.Copy, -SIXTEENTH)
        hi16_1 = weave("hi16_1", na1, whole, ACT.Relu, -SIXTEENTH)
        lo16_0 = lower("lo16_0", pa16_0)
        pb1 = keep.tile([P, PACK, half], F32, name="pb1", tag="pb", align_bytes=64)
        difference(pb1, n2_t, 1, 0)
        mid16_0 = combine("mid16_0", pb16_0, lo16_0, ALU.max)
        for t in range(1, PACK):
            difference(pb1, n2_t, 1, t)
        quarter = half // 2
        pb16_1 = [weave(f"pb16_1{u}", pb1, slice(u * quarter, (u + 1) * quarter), ACT.Copy, SIXTEENTH) for u in range(2)]
        z16_0 = combine("z16_0", mid16_0, hi16_0, ALU.min)
        lo16_1 = lower("lo16_1", pa16_1)
        score(0, z16_0)
        for t in range(PACK):
            empty(0, t)
        parts = [slice(u * quarter * PACK, (u + 1) * quarter * PACK) for u in range(2)]
        mid16_1 = [combine(f"mid16_1{u}", pb16_1[u], lo16_1[:, parts[u]], ALU.max) for u in range(2)]
        z16_1 = [combine(f"z16_1{u}", mid16_1[u], hi16_1[:, parts[u]], ALU.min) for u in range(2)]
        for u in range(2):
            score(half + u * quarter, z16_1[u])

        out_rows = out.rearrange("(g t e) j -> t g e j", t=PACK, e=8)
        pa2 = [keep.tile([P, W], F32, name=f"pa2_{t}", align_bytes=64) for t in range(PACK)]
        gate = [keep.tile([P, W], F32, name=f"gate{t}", align_bytes=64) for t in range(PACK)]

        def fetch_pair(t):
            nc.scalar.activation(gate[t][:], s_rows[t][:].indirect(n4_t[:]), ACT.Sigmoid)
            nc.vector.tensor_copy(pa2[t][:], s_rows[t][:].indirect(n3_t[:]))

        empty(1, 0)
        empty(1, 1)
        fetch_pair(0)
        for t in range(PACK):
            if t + 2 < PACK:
                empty(1, t + 2)
            if t + 1 < PACK:
                fetch_pair(t + 1)
            nc.vector.tensor_tensor(s_rows[t][:].indirect(n4_t[:]), pa2[t][:], gate[t][:], ALU.mult)
            nc.sync.dma_start(out_rows[t], s_rows[t][:])
